import numpy as np
import ml_dtypes


def mxq(x, axis, fmt="e4m3"):
    dtype, down = {"e4m3": (ml_dtypes.float8_e4m3fn, 7), "e5m2": (ml_dtypes.float8_e5m2, 14)}[fmt]
    v = np.moveaxis(np.asarray(x, np.float32).astype(ml_dtypes.bfloat16).astype(np.float64), axis, -1)
    blocks = v.reshape(v.shape[:-1] + (-1, 32))
    amax = np.abs(blocks).max(-1, keepdims=True)
    byte = np.maximum(np.where(amax > 0, np.frexp(amax)[1] - 1 + 127, 0) - down, 1)
    scale = np.exp2(byte - 127.0)
    codes = (blocks / scale).astype(np.float32).astype(dtype).astype(np.float64)
    return np.moveaxis((codes * scale).reshape(v.shape), -1, axis)


WIDE = False


def mx_kscale(k):
    if not WIDE:
        return np.ones(k)
    levels = np.array([10, -10, 5, -5, 0])
    if k % 512:
        return np.exp2(np.random.permutation(np.resize(levels, k // 32))).repeat(32)
    a = np.empty((k // 512, 16))
    for p in range(k // 512):
        a[p, :8] = np.random.permutation(np.resize(levels, 8))
        for g in range(8):
            far = levels[np.abs(levels - a[p, g]) >= 10]
            a[p, g + 8] = far[np.random.randint(len(far))]
    return np.exp2(a.ravel()).repeat(32)


def f64(x):
    return np.asarray(x).astype(np.float64)


def striped(idx):
    return np.tile(idx.reshape(-1, 16).T, (8, 1)).astype(np.uint16)


def unstriped(offs):
    return offs[:16].T.reshape(-1).astype(np.int64)


def striped8(idx):
    return np.concatenate([x.reshape(-1, 16).T for x in idx]).astype(np.uint16)


def runs(offs, k):
    lists = np.stack([offs[16 * r : 16 * r + 16].T.reshape(-1) for r in range(8)]).astype(np.int64)
    return lists[np.arange(k) % 512 // 64]


def pack_weight(w):
    k, n = w.shape
    w = f64(np.asarray(w, np.float32).astype(ml_dtypes.bfloat16)).reshape(k // 32, 32, n)
    amax = np.abs(w).max(1)
    byte = np.clip(np.where(amax > 0, np.frexp(amax)[1] - 1 + 127 - 7, 1), 1, 254)
    scaled = (w * np.exp2(127.0 - byte)[:, None, :]).reshape(k, n).astype(np.float32)
    words = np.ascontiguousarray(scaled.reshape(k // 512, 128, 4, n).transpose(0, 1, 3, 2)).astype(ml_dtypes.float8_e4m3fn).view(np.uint8)
    return words, np.ascontiguousarray(byte.astype(np.uint8).reshape(k // 512, 16, n))


def unpack_weight(words, scales):
    g, p, n, _ = words.shape
    vals = np.ascontiguousarray(words).view(ml_dtypes.float8_e4m3fn).astype(np.float64) * np.repeat(np.exp2(scales.astype(np.float64) - 127.0), 8, axis=1)[..., None]
    return vals.transpose(0, 1, 3, 2).reshape(g * 512, n)


def relu(v):
    return np.maximum(v, 0.0)


K, T, S, H, J, G = 512, 2048, 512, 512, 512, 2048


def setup_inputs():
    n = np.random.standard_normal
    s = mx_kscale(K)[:, None]
    packed_xT = pack_weight(n((K, T)) * s)
    packed_dT = pack_weight(n((K, G)) / s)
    return {
        "x_words": packed_xT[0],
        "x_scales": packed_xT[1],
        "w1": (n((K, H)) / np.sqrt(K) / s).astype(np.float32),
        "tab": n((H, J)).astype(np.float32),
        "gs": (np.random.uniform(0.5, 1.5, (K, 1)) * s).astype(np.float32),
        "d_words": packed_dT[0],
        "d_scales": packed_dT[1],
        "offs": striped(np.random.permutation(T)[:S]),
        "n1": striped8(np.random.randint(0, J, (8, S))),
        "n2": striped8(np.stack([np.random.permutation(S) for _ in range(8)])),
        "k1": striped8(np.random.randint(0, G, (8, H))),
        "n3": striped8(np.stack([np.random.permutation(S) for _ in range(8)])),
        "n4": striped8(np.stack([np.random.permutation(S) for _ in range(8)])),
    }


def reference(x_words, x_scales, w1, tab, gs, d_words, d_scales, offs, n1, n2, k1, n3, n4):
    d_k1 = unpack_weight(d_words, d_scales)[np.arange(K)[:, None], runs(k1, K)]
    xq = unpack_weight(x_words, x_scales)[:, unstriped(offs)]
    y = mxq(f64(w1), 0, "e4m3").T @ xq
    z = f64(gs) * (np.abs(y - (y[np.arange(H)[:, None], runs(n2, H)]) - (f64(tab)[np.arange(H)[:, None], runs(n1, H)])))
    h = 0.0625 * ((d_k1.T @ mxq(z, 0, "e4m3")))
    return relu(h - (h[np.arange(H)[:, None], runs(n3, H)])) + 0.5 * (relu(h[np.arange(H)[:, None], runs(n4, H)] - h))

@@ -1,0 +1,256 @@
+from contextlib import ExitStack
+
+import concourse.mybir as mybir
+
+K, T, S, H, J, G = 512, 2048, 512, 512, 512, 2048
+FLOPS = 2 * K * H * S + 2 * H * H * S
+
+F32 = mybir.dt.float32
+BF16 = mybir.dt.bfloat16
+I32 = mybir.dt.int32
+U32 = mybir.dt.uint32
+U16 = mybir.dt.uint16
+U8 = mybir.dt.uint8
+FP8X4 = mybir.dt.float8_e4m3fn_x4
+ALU = mybir.AluOpType
+ACT = mybir.ActivationFunctionType
+
+P = 128
+PACK = 4
+HALF = S // 2
+QUARTER = S // 4
+
+
+def entries(offsets, part):
+    return offsets[:, part.start // 16 : part.stop // 16]
+
+
+def tile_picked_densekinddhinge_none_p_kernel(
+    tc, x_words, x_scales, w1, tab, gs, d_words, d_scales, offs, n1, n2, k1, n3, n4, out
+):
+    nc = tc.nc
+    with ExitStack() as ctx:
+        keep = ctx.enter_context(tc.tile_pool(name="keep", bufs=1))
+        psum = ctx.enter_context(tc.psum_pool(name="psum", bufs=1))
+
+        def sb(shape, dtype, name, tag=None):
+            return keep.tile(shape, dtype, name=name, tag=tag or name, align_bytes=64)
+
+        def bank(number, width, name):
+            return psum.tile([P, width], F32, name=name, tag="bank%d" % number)
+
+        lists = {}
+
+        def load_list(name, dram):
+            lists[name] = sb([P, S // 16], U16, name + "_list")
+            nc.sync.dma_start(lists[name][:], dram)
+
+        halves = (slice(0, HALF), slice(HALF, S))
+
+        x_bytes = sb([P, T], U8, "x_bytes")
+        d_bytes = sb([P, G], U8, "d_bytes")
+        nc.gpsimd.memset(x_bytes[:].bitcast(I32), 0)
+        nc.vector.memset(d_bytes[:].bitcast(I32), 0)
+
+        w_raw = sb([P, PACK, H], F32, "w_raw")
+        x_table = sb([P, T], U32, "x_table")
+        d_table = sb([P, G], U32, "d_table")
+        gain = sb([P, PACK], F32, "gain")
+        tabs = [sb([P, J], F32, "tab%d" % t) for t in range(PACK)]
+
+        load_list("offs", offs)
+        x_rows = x_scales[0].rearrange("(q r) c -> r q c", r=4)
+        for r in range(4):
+            nc.scalar.dma_start(x_bytes[r:P:32, :].bitcast(I32), x_rows[r].bitcast(I32))
+        nc.sync.dma_start(w_raw[:], w1.rearrange("(p j) c -> p j c", j=PACK))
+        load_list("k1", k1)
+        d_rows = d_scales[0].rearrange("(r e) c -> e r c", e=2)
+        for e in range(2):
+            nc.scalar.dma_start(d_bytes[e:P:16, :].bitcast(I32), d_rows[e].bitcast(I32))
+        load_list("n1", n1)
+        load_list("n2", n2)
+        nc.sync.dma_start(x_table[:].bitcast(I32), x_words[0].rearrange("p n t -> p (n t)").bitcast(I32))
+        nc.scalar.dma_start(gain[:], gs.rearrange("(p t) o -> p (t o)", t=PACK))
+        tab_rows = tab.rearrange("(p t) c -> t p c", t=PACK)
+        for t in range(PACK):
+            nc.sync.dma_start(tabs[t][:], tab_rows[t])
+        nc.sync.dma_start(d_table[:].bitcast(I32), d_words[0].rearrange("p n t -> p (n t)").bitcast(I32))
+        load_list("n3", n3)
+        load_list("n4", n4)
+
+        xq_bytes = sb([P, S], U8, "xq_bytes")
+        nc.vector.tensor_copy(xq_bytes[:], x_bytes[:].indirect(lists["offs"][:]))
+
+        w_bf = sb([P, PACK * H], BF16, "w_bf")
+        w_dst = w_bf[:].rearrange("p (t m j) -> p m t j", t=PACK, j=PACK)
+        w_src = w_raw[:].rearrange("p j (m t) -> p m t j", t=PACK)
+        nc.vector.tensor_copy(w_dst[:, 0:80], w_src[:, 0:80])
+        nc.scalar.activation(w_dst[:, 80:128], w_src[:, 80:128], ACT.Copy)
+
+        w_codes = sb([P, H], U32, "w_codes")
+        w_plane = sb([P, H], U8, "w_plane")
+        nc.vector.quantize_mx(out=w_codes[:].bitcast(FP8X4), scales=w_plane[:], in_=w_bf[:])
+
+        xq_words = sb([P, S], U32, "xq_words")
+        for part in halves:
+            nc.vector.tensor_copy(xq_words[:, part], x_table[:].indirect(entries(lists["offs"], part)))
+
+        dq_bytes = sb([P, H], U8, "dq_bytes")
+        nc.vector.tensor_copy(dq_bytes[:], d_bytes[:].indirect(lists["k1"][:]))
+        d_dealt = sb([P, H], U8, "d_dealt")
+        d_plane = sb([P, H], U8, "d_plane")
+        for dst in (d_dealt, d_plane):
+            nc.vector.tensor_copy(
+                dst[:].rearrange("p (t m) -> p m t", t=PACK), dq_bytes[:].rearrange("p (m t) -> p m t", t=PACK)
+            )
+        for e in range(2):
+            nc.sync.dma_start(d_plane[2 + e : P : 32, :].bitcast(I32), d_dealt[16 + e : P : 32, :].bitcast(I32))
+
+        ys = [sb([P, S], F32, "y%d" % t) for t in range(PACK)]
+        for pair in range(2):
+            for c, part in enumerate(halves):
+                for t in (2 * pair, 2 * pair + 1):
+                    cols = slice(t * P, (t + 1) * P)
+                    acc = bank(2 * t + c, HALF, "y_acc%d_%d" % (t, c))
+                    nc.tensor.matmul_mx(
+                        out=acc[:],
+                        lhsT=w_codes[:, cols].bitcast(FP8X4),
+                        lhsT_scale=w_plane[:, cols],
+                        rhs=xq_words[:, part].bitcast(FP8X4),
+                        rhs_scale=xq_bytes[:, part],
+                        start=True,
+                        stop=True,
+                    )
+                    nc.scalar.activation(ys[t][:, part], acc[:], ACT.Copy)
+
+        z_codes = sb([P, S], U32, "z_codes")
+        z_plane = sb([P, S], U8, "z_plane")
+        z = sb([P, PACK, S], F32, "z")
+        z_bf = sb([P, PACK * S], BF16, "z_bf")
+
+        def sizes(pair, part, tag=None):
+            count = part.stop - part.start
+            name = "_%d_%d" % (pair, part.start)
+            less_y = sb([P, 2, count], F32, "less_y" + name, tag)
+            diff = sb([P, 2, count], F32, "diff" + name)
+            size = sb([P, 2, count], F32, "size" + name)
+            for u in range(2):
+                t = 2 * pair + u
+                nc.vector.tensor_tensor(
+                    less_y[:, u, :], tabs[t][:].indirect(entries(lists["n1"], part)), ys[t][:, part], ALU.subtract
+                )
+            for u in range(2):
+                t = 2 * pair + u
+                nc.vector.tensor_tensor(
+                    diff[:, u, :], ys[t][:].indirect(entries(lists["n2"], part)), less_y[:, u, :], ALU.add
+                )
+            nc.scalar.activation(size[:], diff[:], ACT.Abs)
+            for u in range(2):
+                t = 2 * pair + u
+                nc.scalar.activation(z[:, t, part], size[:, u, :], ACT.Copy, scale=gain[:, t : t + 1])
+
+        def weave(part):
+            nc.scalar.copy(
+                z_bf[:, PACK * part.start : PACK * part.stop].rearrange("p (c i t) -> p c t i", i=4, t=PACK),
+                z[:, :, part].rearrange("p t (c i) -> p c t i", i=4),
+            )
+
+        def quantise(part):
+            nc.vector.quantize_mx(
+                out=z_codes[:, part].bitcast(FP8X4),
+                scales=z_plane[:, part],
+                in_=z_bf[:, PACK * part.start : PACK * part.stop],
+            )
+
+        third = slice(HALF, HALF + QUARTER)
+        last = slice(HALF + QUARTER, S)
+        sizes(0, halves[0])
+        sizes(1, halves[0])
+        weave(halves[0])
+        sizes(0, halves[1])
+        sizes(1, third, "late")
+        weave(third)
+        quantise(halves[0])
+        sizes(1, last)
+        weave(last)
+
+        dq_words = sb([P, H], U32, "dq_words", "late")
+        nc.vector.tensor_copy(dq_words[:], d_table[:].indirect(lists["k1"][:]))
+        quantise(third)
+        d_codes = sb([P, H], U32, "d_codes")
+        nc.vector.tensor_copy(
+            d_codes[:].bitcast(I32).rearrange("p (t m) -> p m t", t=PACK),
+            dq_words[:].bitcast(I32).rearrange("p (m t) -> p m t", t=PACK),
+        )
+        quantise(last)
+
+        out_rows = out.rearrange("(p t) c -> t p c", t=PACK)
+        wide = {t: sb([P, 2 * S], F32, "h_wide%d" % t) for t in (1, 2)}
+        windows = [sb([P, S], F32, "h_window0"), wide[1], wide[2], sb([P, S], F32, "h_window3")]
+        plain2 = sb([P, S], F32, "h_plain2")
+        plain3 = sb([P, S], F32, "h_plain3")
+        plains = [wide[1][:, S:], wide[2][:, S:], plain2[:], plain3[:]]
+
+        def product(t, part, number):
+            cols = slice(t * P, (t + 1) * P)
+            acc = bank(number, part.stop - part.start, "h_acc%d_%d" % (t, part.start))
+            nc.tensor.matmul_mx(
+                out=acc[:],
+                lhsT=d_codes[:, cols].bitcast(FP8X4),
+                lhsT_scale=d_plane[:, cols],
+                rhs=z_codes[:, part].bitcast(FP8X4),
+                rhs_scale=z_plane[:, part],
+                start=True,
+                stop=True,
+            )
+            return acc
+
+        firsts = [(part, product(0, part, i)) for i, part in enumerate((halves[0], third, last))]
+        for part, acc in firsts[:2]:
+            nc.scalar.activation(windows[0][:, part], acc[:], ACT.Copy, scale=0.03125)
+        nc.vector.tensor_scalar(windows[0][:, last], firsts[2][1][:], 0.03125, None, ALU.mult)
+        for part, acc in firsts:
+            nc.scalar.activation(plains[0][:, part], acc[:], ACT.Copy, scale=0.03125)
+        whole = slice(0, S)
+
+        def fetch(t):
+            acc = product(t, whole, 2 + t)
+            nc.scalar.activation(windows[t][:, whole], acc[:], ACT.Copy, scale=0.03125)
+            nc.scalar.activation(plains[t], acc[:], ACT.Copy, scale=0.03125)
+
+        pieces = {0: halves, 1: (whole,), 2: (whole,), 3: halves}
+        pending = None
+        for t in range(PACK):
+            if t + 1 < PACK:
+                fetch(t + 1)
+            down = sb([P, S], F32, "down%d" % t)
+            up = sb([P, S], F32, "up%d" % t)
+            hinge = sb([P, S], F32, "hinge%d" % t)
+            result = sb([P, S], F32, "result%d" % t)
+            for part in pieces[t]:
+                nc.vector.tensor_tensor(
+                    down[:, part], windows[t][:].indirect(entries(lists["n3"], part)), plains[t][:, part], ALU.subtract
+                )
+            nc.scalar.activation(hinge[:], down[:], ACT.Relu, scale=-2.0)
+
+            def finish(part, t=t, up=up, hinge=hinge, result=result):
+                nc.vector.scalar_tensor_tensor(result[:, part], up[:, part], 0.0, hinge[:, part], ALU.max, ALU.add)
+                nc.sync.dma_start(out_rows[t][:, part], result[:, part])
+
+            if pending is not None:
+                pending(whole)
+            if t + 1 < PACK:
+                for part in pieces[t]:
+                    nc.vector.tensor_tensor(
+                        up[:, part], windows[t][:].indirect(entries(lists["n4"], part)), plains[t][:, part], ALU.subtract
+                    )
+                pending = finish
+            else:
+                tail = (halves[0], third, last)
+                for i, part in enumerate(tail):
+                    nc.vector.tensor_tensor(
+                        up[:, part], windows[t][:].indirect(entries(lists["n4"], part)), plains[t][:, part], ALU.subtract
+                    )
+                    if i > 0:
+                        finish(tail[i - 1])
+                finish(last)

@@ -49,8 +49,12 @@ def tile_picked_densekinddhinge_none_p_kernel(
 
         x_bytes = sb([P, T], U8, "x_bytes")
         d_bytes = sb([P, G], U8, "d_bytes")
-        nc.gpsimd.memset(x_bytes[:].bitcast(I32), 0)
-        nc.vector.memset(d_bytes[:].bitcast(I32), 0)
+        d_plane = sb([P, H], U8, "d_plane")
+        nc.gpsimd.memset(x_bytes[:, : T // 2].bitcast(I32), 0)
+        nc.vector.memset(x_bytes[:, T // 2 :].bitcast(I32), 0)
+        nc.gpsimd.memset(d_bytes[:, : G // 2].bitcast(I32), 0)
+        nc.vector.memset(d_bytes[:, G // 2 :].bitcast(I32), 0)
+        nc.gpsimd.memset(d_plane[:].bitcast(I32), 0)
 
         w_raw = sb([P, PACK, H], F32, "w_raw")
         x_table = sb([P, T], U32, "x_table")
@@ -59,17 +63,17 @@ def tile_picked_densekinddhinge_none_p_kernel(
         tabs = [sb([P, J], F32, "tab%d" % t) for t in range(PACK)]
 
         load_list("offs", offs)
+        load_list("k1", k1)
         x_rows = x_scales[0].rearrange("(q r) c -> r q c", r=4)
         for r in range(4):
-            nc.scalar.dma_start(x_bytes[r:P:32, :].bitcast(I32), x_rows[r].bitcast(I32))
-        nc.sync.dma_start(w_raw[:], w1.rearrange("(p j) c -> p j c", j=PACK))
-        load_list("k1", k1)
+            nc.sync.dma_start(x_bytes[r:P:32, :].bitcast(I32), x_rows[r].bitcast(I32))
         d_rows = d_scales[0].rearrange("(r e) c -> e r c", e=2)
         for e in range(2):
-            nc.scalar.dma_start(d_bytes[e:P:16, :].bitcast(I32), d_rows[e].bitcast(I32))
+            nc.sync.dma_start(d_bytes[e:P:16, :].bitcast(I32), d_rows[e].bitcast(I32))
+        nc.sync.dma_start(w_raw[:], w1.rearrange("(p j) c -> p j c", j=PACK))
+        nc.sync.dma_start(x_table[:].bitcast(I32), x_words[0].rearrange("p n t -> p (n t)").bitcast(I32))
         load_list("n1", n1)
         load_list("n2", n2)
-        nc.sync.dma_start(x_table[:].bitcast(I32), x_words[0].rearrange("p n t -> p (n t)").bitcast(I32))
         nc.scalar.dma_start(gain[:], gs.rearrange("(p t) o -> p (t o)", t=PACK))
         tab_rows = tab.rearrange("(p t) c -> t p c", t=PACK)
         for t in range(PACK):
@@ -81,30 +85,31 @@ def tile_picked_densekinddhinge_none_p_kernel(
         xq_bytes = sb([P, S], U8, "xq_bytes")
         nc.vector.tensor_copy(xq_bytes[:], x_bytes[:].indirect(lists["offs"][:]))
 
-        w_bf = sb([P, PACK * H], BF16, "w_bf")
-        w_dst = w_bf[:].rearrange("p (t m j) -> p m t j", t=PACK, j=PACK)
+        dq_bytes = sb([P, H], U8, "dq_bytes", "early")
+        nc.vector.tensor_copy(dq_bytes[:], d_bytes[:].indirect(lists["k1"][:]))
+        d_dealt = sb([P, H], U8, "d_dealt")
+        nc.vector.tensor_copy(
+            d_dealt[:].rearrange("p (t m) -> p t m", t=PACK), dq_bytes[:].rearrange("p (m t) -> p t m", t=PACK)
+        )
+        for odd in range(2):
+            for e in range(2):
+                nc.sync.dma_start(
+                    d_plane[2 * odd + e : P : 32, :].bitcast(I32), d_dealt[16 * odd + e : P : 32, :].bitcast(I32)
+                )
+
         w_src = w_raw[:].rearrange("p j (m t) -> p m t j", t=PACK)
-        nc.vector.tensor_copy(w_dst[:, 0:80], w_src[:, 0:80])
-        nc.scalar.activation(w_dst[:, 80:128], w_src[:, 80:128], ACT.Copy)
+        w_bfs = [sb([P, 2 * H], BF16, "w_bf0", "early"), sb([P, 2 * H], BF16, "w_bf1")]
+        w_dsts = [w_bf[:].rearrange("p (t m j) -> p m t j", t=2, j=PACK) for w_bf in w_bfs]
+        nc.vector.tensor_copy(w_dsts[0], w_src[:, :, 0:2, :])
+        nc.scalar.activation(w_dsts[1], w_src[:, :, 2:4, :], ACT.Copy)
 
         w_codes = sb([P, H], U32, "w_codes")
         w_plane = sb([P, H], U8, "w_plane")
-        nc.vector.quantize_mx(out=w_codes[:].bitcast(FP8X4), scales=w_plane[:], in_=w_bf[:])
-
         xq_words = sb([P, S], U32, "xq_words")
+        nc.vector.quantize_mx(out=w_codes[:, halves[0]].bitcast(FP8X4), scales=w_plane[:, halves[0]], in_=w_bfs[0][:])
         for part in halves:
             nc.vector.tensor_copy(xq_words[:, part], x_table[:].indirect(entries(lists["offs"], part)))
-
-        dq_bytes = sb([P, H], U8, "dq_bytes")
-        nc.vector.tensor_copy(dq_bytes[:], d_bytes[:].indirect(lists["k1"][:]))
-        d_dealt = sb([P, H], U8, "d_dealt")
-        d_plane = sb([P, H], U8, "d_plane")
-        for dst in (d_dealt, d_plane):
-            nc.vector.tensor_copy(
-                dst[:].rearrange("p (t m) -> p m t", t=PACK), dq_bytes[:].rearrange("p (m t) -> p m t", t=PACK)
-            )
-        for e in range(2):
-            nc.sync.dma_start(d_plane[2 + e : P : 32, :].bitcast(I32), d_dealt[16 + e : P : 32, :].bitcast(I32))
+        nc.vector.quantize_mx(out=w_codes[:, halves[1]].bitcast(FP8X4), scales=w_plane[:, halves[1]], in_=w_bfs[1][:])
 
         ys = [sb([P, S], F32, "y%d" % t) for t in range(PACK)]
         for pair in range(2):
@@ -179,8 +184,8 @@ def tile_picked_densekinddhinge_none_p_kernel(
         quantise(third)
         d_codes = sb([P, H], U32, "d_codes")
         nc.vector.tensor_copy(
-            d_codes[:].bitcast(I32).rearrange("p (t m) -> p m t", t=PACK),
-            dq_words[:].bitcast(I32).rearrange("p (m t) -> p m t", t=PACK),
+            d_codes[:].bitcast(I32).rearrange("p (t c i) -> p c t i", t=PACK, i=4),
+            dq_words[:].bitcast(I32).rearrange("p (c i t) -> p c t i", t=PACK, i=4),
         )
         quantise(last)
 
@@ -233,8 +238,13 @@ def tile_picked_densekinddhinge_none_p_kernel(
                 )
             nc.scalar.activation(hinge[:], down[:], ACT.Relu, scale=-2.0)
 
-            def finish(part, t=t, up=up, hinge=hinge, result=result):
-                nc.vector.scalar_tensor_tensor(result[:, part], up[:, part], 0.0, hinge[:, part], ALU.max, ALU.add)
+            rise = sb([P, S], F32, "rise%d" % t)
+
+            def finish(part, t=t, up=up, hinge=hinge, result=result, rise=rise):
+                if t + 1 < PACK:
+                    nc.vector.tensor_tensor(result[:, part], rise[:, part], hinge[:, part], ALU.add)
+                else:
+                    nc.vector.scalar_tensor_tensor(result[:, part], up[:, part], 0.0, hinge[:, part], ALU.max, ALU.add)
                 nc.sync.dma_start(out_rows[t][:, part], result[:, part])
 
             if pending is not None:
@@ -244,6 +254,7 @@ def tile_picked_densekinddhinge_none_p_kernel(
                     nc.vector.tensor_tensor(
                         up[:, part], windows[t][:].indirect(entries(lists["n4"], part)), plains[t][:, part], ALU.subtract
                     )
+                nc.scalar.activation(rise[:], up[:], ACT.Relu)
                 pending = finish
             else:
                 tail = (halves[0], third, last)

@@ -1,6 +1,7 @@
 from contextlib import ExitStack
 
 import concourse.mybir as mybir
+from concourse.masks import make_identity
 
 K, T, S, H, J, G = 512, 2048, 512, 512, 512, 2048
 FLOPS = 2 * K * H * S + 2 * H * H * S
@@ -17,12 +18,27 @@ ACT = mybir.ActivationFunctionType
 
 P = 128
 PACK = 4
-HALF = S // 2
-QUARTER = S // 4
+GROUP = 16
+LINE = 4
+
+WHOLE = slice(0, S)
+FIRST_HALF = slice(0, S // 2)
+SECOND_HALF = slice(S // 2, S)
+THIRD_QUARTER = slice(S // 2, 3 * S // 4)
+LAST_QUARTER = slice(3 * S // 4, S)
+HALVES = (FIRST_HALF, SECOND_HALF)
+TAPER = (FIRST_HALF, THIRD_QUARTER, LAST_QUARTER)
+BLOCKS = tuple(slice(c * P, (c + 1) * P) for c in range(S // P))
+
+HALF_H_SCALE = 0.0625 * 0.5
+
+
+def width(part):
+    return part.stop - part.start
 
 
 def entries(offsets, part):
-    return offsets[:, part.start // 16 : part.stop // 16]
+    return offsets[:, part.start // GROUP : part.stop // GROUP]
 
 
 def tile_picked_densekinddhinge_none_p_kernel(
@@ -33,112 +49,109 @@ def tile_picked_densekinddhinge_none_p_kernel(
         keep = ctx.enter_context(tc.tile_pool(name="keep", bufs=1))
         psum = ctx.enter_context(tc.psum_pool(name="psum", bufs=1))
 
-        def sb(shape, dtype, name, tag=None):
-            return keep.tile(shape, dtype, name=name, tag=tag or name, align_bytes=64)
+        def sbuf(shape, dtype, name, slot=None):
+            return keep.tile(shape, dtype, name=name, tag=slot or name, align_bytes=64)
 
-        def bank(number, width, name):
-            return psum.tile([P, width], F32, name=name, tag="bank%d" % number)
+        def bank(number, columns, name):
+            return psum.tile([P, columns], F32, name=name, tag="bank%d" % number)
+
+        def product(acc, stationary, stationary_plane, moving, moving_plane):
+            nc.tensor.matmul_mx(
+                out=acc,
+                lhsT=stationary.bitcast(FP8X4),
+                lhsT_scale=stationary_plane,
+                rhs=moving.bitcast(FP8X4),
+                rhs_scale=moving_plane,
+                start=True,
+                stop=True,
+            )
 
         lists = {}
 
         def load_list(name, dram):
-            lists[name] = sb([P, S // 16], U16, name + "_list")
+            lists[name] = sbuf([P, S // GROUP], U16, name + "_list")
             nc.sync.dma_start(lists[name][:], dram)
 
-        halves = (slice(0, HALF), slice(HALF, S))
-
-        x_bytes = sb([P, T], U8, "x_bytes")
-        d_bytes = sb([P, G], U8, "d_bytes")
-        d_plane = sb([P, H], U8, "d_plane")
-        nc.gpsimd.memset(x_bytes[:, : T // 2].bitcast(I32), 0)
-        nc.vector.memset(x_bytes[:, T // 2 :].bitcast(I32), 0)
-        nc.gpsimd.memset(d_bytes[:, : G // 2].bitcast(I32), 0)
-        nc.vector.memset(d_bytes[:, G // 2 :].bitcast(I32), 0)
+        x_bytes = sbuf([P, T], U8, "x_bytes")
+        d_bytes = sbuf([P, G], U8, "d_bytes")
+        d_plane = sbuf([P, H], U8, "d_plane")
+        for table_bytes in (x_bytes, d_bytes):
+            nc.gpsimd.memset(table_bytes[:, : T // 2].bitcast(I32), 0)
+            nc.vector.memset(table_bytes[:, T // 2 :].bitcast(I32), 0)
         nc.gpsimd.memset(d_plane[:].bitcast(I32), 0)
+        identity = sbuf([P, P], F32, "identity")
+        make_identity(nc, identity[:])
 
-        w_raw = sb([P, PACK, H], F32, "w_raw")
-        x_table = sb([P, T], U32, "x_table")
-        d_table = sb([P, G], U32, "d_table")
-        gain = sb([P, PACK], F32, "gain")
-        tabs = [sb([P, J], F32, "tab%d" % t) for t in range(PACK)]
+        w_raw = sbuf([P, PACK, H], F32, "w_raw")
+        x_table = sbuf([P, T], U32, "x_table")
+        d_table = sbuf([P, G], U32, "d_table")
+        gain = sbuf([P, PACK], F32, "gain")
+        tabs = [sbuf([P, J], F32, "tab%d" % t) for t in range(PACK)]
 
         load_list("offs", offs)
         load_list("k1", k1)
-        x_rows = x_scales[0].rearrange("(q r) c -> r q c", r=4)
-        for r in range(4):
-            nc.sync.dma_start(x_bytes[r:P:32, :].bitcast(I32), x_rows[r].bitcast(I32))
-        d_rows = d_scales[0].rearrange("(r e) c -> e r c", e=2)
-        for e in range(2):
-            nc.sync.dma_start(d_bytes[e:P:16, :].bitcast(I32), d_rows[e].bitcast(I32))
+        x_rows = x_scales[0].rearrange("(q a) c -> a q c", a=4)
+        for a in range(4):
+            nc.sync.dma_start(x_bytes[a:P:32, :].bitcast(I32), x_rows[a].bitcast(I32))
+        nc.sync.dma_start(d_bytes[0:P:8, :].bitcast(I32), d_scales[0].bitcast(I32))
         nc.sync.dma_start(w_raw[:], w1.rearrange("(p j) c -> p j c", j=PACK))
         nc.sync.dma_start(x_table[:].bitcast(I32), x_words[0].rearrange("p n t -> p (n t)").bitcast(I32))
         load_list("n1", n1)
         load_list("n2", n2)
-        nc.scalar.dma_start(gain[:], gs.rearrange("(p t) o -> p (t o)", t=PACK))
         tab_rows = tab.rearrange("(p t) c -> t p c", t=PACK)
         for t in range(PACK):
             nc.sync.dma_start(tabs[t][:], tab_rows[t])
+        nc.sync.dma_start(gain[:], gs.rearrange("(p t) o -> p (t o)", t=PACK))
         nc.sync.dma_start(d_table[:].bitcast(I32), d_words[0].rearrange("p n t -> p (n t)").bitcast(I32))
         load_list("n3", n3)
         load_list("n4", n4)
 
-        xq_bytes = sb([P, S], U8, "xq_bytes")
-        nc.vector.tensor_copy(xq_bytes[:], x_bytes[:].indirect(lists["offs"][:]))
+        x_plane = sbuf([P, S], U8, "x_plane")
+        nc.vector.tensor_copy(x_plane[:], x_bytes[:].indirect(lists["offs"][:]))
 
-        dq_bytes = sb([P, H], U8, "dq_bytes", "early")
-        nc.vector.tensor_copy(dq_bytes[:], d_bytes[:].indirect(lists["k1"][:]))
-        d_dealt = sb([P, H], U8, "d_dealt")
+        d_picked_bytes = sbuf([P, H], U8, "d_picked_bytes", "before_w_cast")
+        nc.vector.tensor_copy(d_picked_bytes[:], d_bytes[:].indirect(lists["k1"][:]))
+        d_dealt_bytes = sbuf([P, H], U8, "d_dealt_bytes")
         nc.vector.tensor_copy(
-            d_dealt[:].rearrange("p (t m) -> p t m", t=PACK), dq_bytes[:].rearrange("p (m t) -> p t m", t=PACK)
+            d_dealt_bytes[:].rearrange("p (t m) -> p t m", t=PACK),
+            d_picked_bytes[:].rearrange("p (m t) -> p t m", t=PACK),
         )
-        for odd in range(2):
-            for e in range(2):
-                nc.sync.dma_start(
-                    d_plane[2 * odd + e : P : 32, :].bitcast(I32), d_dealt[16 * odd + e : P : 32, :].bitcast(I32)
-                )
 
         w_src = w_raw[:].rearrange("p j (m t) -> p m t j", t=PACK)
-        w_bfs = [sb([P, 2 * H], BF16, "w_bf0", "early"), sb([P, 2 * H], BF16, "w_bf1")]
+        w_bfs = [sbuf([P, 2 * H], BF16, "w_bf0", "before_w_cast"), sbuf([P, 2 * H], BF16, "w_bf1")]
         w_dsts = [w_bf[:].rearrange("p (t m j) -> p m t j", t=2, j=PACK) for w_bf in w_bfs]
         nc.vector.tensor_copy(w_dsts[0], w_src[:, :, 0:2, :])
         nc.scalar.activation(w_dsts[1], w_src[:, :, 2:4, :], ACT.Copy)
 
-        w_codes = sb([P, H], U32, "w_codes")
-        w_plane = sb([P, H], U8, "w_plane")
-        xq_words = sb([P, S], U32, "xq_words")
-        nc.vector.quantize_mx(out=w_codes[:, halves[0]].bitcast(FP8X4), scales=w_plane[:, halves[0]], in_=w_bfs[0][:])
-        for part in halves:
-            nc.vector.tensor_copy(xq_words[:, part], x_table[:].indirect(entries(lists["offs"], part)))
-        nc.vector.quantize_mx(out=w_codes[:, halves[1]].bitcast(FP8X4), scales=w_plane[:, halves[1]], in_=w_bfs[1][:])
+        w_codes = sbuf([P, H], U32, "w_codes")
+        w_plane = sbuf([P, H], U8, "w_plane")
+        x_codes = sbuf([P, S], U32, "x_codes")
+        nc.vector.quantize_mx(out=w_codes[:, FIRST_HALF].bitcast(FP8X4), scales=w_plane[:, FIRST_HALF], in_=w_bfs[0][:])
+        for part in HALVES:
+            nc.vector.tensor_copy(x_codes[:, part], x_table[:].indirect(entries(lists["offs"], part)))
+        nc.vector.quantize_mx(out=w_codes[:, SECOND_HALF].bitcast(FP8X4), scales=w_plane[:, SECOND_HALF], in_=w_bfs[1][:])
 
-        ys = [sb([P, S], F32, "y%d" % t) for t in range(PACK)]
+        for a in range(4):
+            nc.sync.dma_start(d_plane[a:P:32, :].bitcast(I32), d_dealt_bytes[8 * a : P : 32, :].bitcast(I32))
+
+        ys = [sbuf([P, S], F32, "y%d" % t) for t in range(PACK)]
         for pair in range(2):
-            for c, part in enumerate(halves):
+            for c, part in enumerate(HALVES):
                 for t in (2 * pair, 2 * pair + 1):
-                    cols = slice(t * P, (t + 1) * P)
-                    acc = bank(2 * t + c, HALF, "y_acc%d_%d" % (t, c))
-                    nc.tensor.matmul_mx(
-                        out=acc[:],
-                        lhsT=w_codes[:, cols].bitcast(FP8X4),
-                        lhsT_scale=w_plane[:, cols],
-                        rhs=xq_words[:, part].bitcast(FP8X4),
-                        rhs_scale=xq_bytes[:, part],
-                        start=True,
-                        stop=True,
-                    )
+                    acc = bank(2 * t + c, width(part), "y_acc%d_%d" % (t, c))
+                    product(acc[:], w_codes[:, BLOCKS[t]], w_plane[:, BLOCKS[t]], x_codes[:, part], x_plane[:, part])
                     nc.scalar.activation(ys[t][:, part], acc[:], ACT.Copy)
 
-        z_codes = sb([P, S], U32, "z_codes")
-        z_plane = sb([P, S], U8, "z_plane")
-        z = sb([P, PACK, S], F32, "z")
-        z_bf = sb([P, PACK * S], BF16, "z_bf")
+        z_codes = sbuf([P, S], U32, "z_codes")
+        z_plane = sbuf([P, S], U8, "z_plane")
+        z = sbuf([P, PACK, S], F32, "z")
+        z_bf = sbuf([P, PACK * S], BF16, "z_bf")
 
-        def sizes(pair, part, tag=None):
-            count = part.stop - part.start
+        def make_z(pair, part, slot=None):
             name = "_%d_%d" % (pair, part.start)
-            less_y = sb([P, 2, count], F32, "less_y" + name, tag)
-            diff = sb([P, 2, count], F32, "diff" + name)
-            size = sb([P, 2, count], F32, "size" + name)
+            less_y = sbuf([P, 2, width(part)], F32, "less_y" + name, slot)
+            diff = sbuf([P, 2, width(part)], F32, "diff" + name)
+            size = sbuf([P, 2, width(part)], F32, "size" + name)
             for u in range(2):
                 t = 2 * pair + u
                 nc.vector.tensor_tensor(
@@ -154,114 +167,124 @@ def tile_picked_densekinddhinge_none_p_kernel(
                 t = 2 * pair + u
                 nc.scalar.activation(z[:, t, part], size[:, u, :], ACT.Copy, scale=gain[:, t : t + 1])
 
-        def weave(part):
+        def round_z(part):
             nc.scalar.copy(
-                z_bf[:, PACK * part.start : PACK * part.stop].rearrange("p (c i t) -> p c t i", i=4, t=PACK),
-                z[:, :, part].rearrange("p t (c i) -> p c t i", i=4),
+                z_bf[:, PACK * part.start : PACK * part.stop].rearrange("p (c i t) -> p c t i", i=LINE, t=PACK),
+                z[:, :, part].rearrange("p t (c i) -> p c t i", i=LINE),
             )
 
-        def quantise(part):
+        def quantise_z(part):
             nc.vector.quantize_mx(
                 out=z_codes[:, part].bitcast(FP8X4),
                 scales=z_plane[:, part],
                 in_=z_bf[:, PACK * part.start : PACK * part.stop],
             )
 
-        third = slice(HALF, HALF + QUARTER)
-        last = slice(HALF + QUARTER, S)
-        sizes(0, halves[0])
-        sizes(1, halves[0])
-        weave(halves[0])
-        sizes(0, halves[1])
-        sizes(1, third, "late")
-        weave(third)
-        quantise(halves[0])
-        sizes(1, last)
-        weave(last)
+        make_z(0, FIRST_HALF)
+        make_z(1, FIRST_HALF)
+        round_z(FIRST_HALF)
+        make_z(0, SECOND_HALF)
+        make_z(1, THIRD_QUARTER, "before_d_words")
+        round_z(THIRD_QUARTER)
+        make_z(1, LAST_QUARTER)
+        round_z(LAST_QUARTER)
 
-        dq_words = sb([P, H], U32, "dq_words", "late")
-        nc.vector.tensor_copy(dq_words[:], d_table[:].indirect(lists["k1"][:]))
-        quantise(third)
-        d_codes = sb([P, H], U32, "d_codes")
-        nc.vector.tensor_copy(
-            d_codes[:].bitcast(I32).rearrange("p (t c i) -> p c t i", t=PACK, i=4),
-            dq_words[:].bitcast(I32).rearrange("p (c i t) -> p c t i", t=PACK, i=4),
-        )
-        quantise(last)
+        d_picked_words = sbuf([P, H], U32, "d_picked_words", "before_d_words")
+        nc.vector.tensor_copy(d_picked_words[:], d_table[:].indirect(lists["k1"][:]))
+        quantise_z(FIRST_HALF)
+        d_codes = sbuf([P, H], U32, "d_codes")
+        deal_dst = d_codes[:].bitcast(I32).rearrange("p (t c i) -> p c t i", t=PACK, i=LINE)
+        deal_src = d_picked_words[:].bitcast(I32).rearrange("p (c i t) -> p c t i", t=PACK, i=LINE)
+        nc.vector.tensor_copy(deal_dst[:, :, 0:1, :], deal_src[:, :, 0:1, :])
+        quantise_z(THIRD_QUARTER)
+        quantise_z(LAST_QUARTER)
+        nc.vector.tensor_copy(deal_dst[:, :, 1:PACK, :], deal_src[:, :, 1:PACK, :])
 
         out_rows = out.rearrange("(p t) c -> t p c", t=PACK)
-        wide = {t: sb([P, 2 * S], F32, "h_wide%d" % t) for t in (1, 2)}
-        windows = [sb([P, S], F32, "h_window0"), wide[1], wide[2], sb([P, S], F32, "h_window3")]
-        plain2 = sb([P, S], F32, "h_plain2")
-        plain3 = sb([P, S], F32, "h_plain3")
+        wide = {t: sbuf([P, 2 * S], F32, "h_wide%d" % t) for t in (1, 2)}
+        windows = [sbuf([P, S], F32, "h_window0"), wide[1], wide[2], sbuf([P, S], F32, "h_window3")]
+        plain2 = sbuf([P, S], F32, "h_plain2")
+        plain3 = sbuf([P, S], F32, "h_plain3")
         plains = [wide[1][:, S:], wide[2][:, S:], plain2[:], plain3[:]]
 
-        def product(t, part, number):
-            cols = slice(t * P, (t + 1) * P)
-            acc = bank(number, part.stop - part.start, "h_acc%d_%d" % (t, part.start))
-            nc.tensor.matmul_mx(
-                out=acc[:],
-                lhsT=d_codes[:, cols].bitcast(FP8X4),
-                lhsT_scale=d_plane[:, cols],
-                rhs=z_codes[:, part].bitcast(FP8X4),
-                rhs_scale=z_plane[:, part],
-                start=True,
-                stop=True,
-            )
+        def second_product(t, part, number):
+            acc = bank(number, width(part), "h_acc%d_%d" % (t, part.start))
+            product(acc[:], d_codes[:, BLOCKS[t]], d_plane[:, BLOCKS[t]], z_codes[:, part], z_plane[:, part])
             return acc
 
-        firsts = [(part, product(0, part, i)) for i, part in enumerate((halves[0], third, last))]
-        for part, acc in firsts[:2]:
-            nc.scalar.activation(windows[0][:, part], acc[:], ACT.Copy, scale=0.03125)
-        nc.vector.tensor_scalar(windows[0][:, last], firsts[2][1][:], 0.03125, None, ALU.mult)
-        for part, acc in firsts:
-            nc.scalar.activation(plains[0][:, part], acc[:], ACT.Copy, scale=0.03125)
-        whole = slice(0, S)
+        first_accs = [second_product(0, part, number) for number, part in enumerate(TAPER)]
+        for part, acc in zip(TAPER[:2], first_accs):
+            nc.scalar.activation(windows[0][:, part], acc[:], ACT.Copy, scale=HALF_H_SCALE)
+        nc.vector.tensor_scalar(windows[0][:, LAST_QUARTER], first_accs[2][:], HALF_H_SCALE, None, ALU.mult)
+        for part, acc in zip(TAPER, first_accs):
+            nc.scalar.activation(plains[0][:, part], acc[:], ACT.Copy, scale=HALF_H_SCALE)
+        for t in range(1, PACK):
+            acc = second_product(t, WHOLE, 2 + t)
+            nc.scalar.activation(windows[t][:, WHOLE], acc[:], ACT.Copy, scale=HALF_H_SCALE)
+            nc.scalar.activation(plains[t], acc[:], ACT.Copy, scale=HALF_H_SCALE)
 
-        def fetch(t):
-            acc = product(t, whole, 2 + t)
-            nc.scalar.activation(windows[t][:, whole], acc[:], ACT.Copy, scale=0.03125)
-            nc.scalar.activation(plains[t], acc[:], ACT.Copy, scale=0.03125)
+        downs = [sbuf([P, S], F32, "down%d" % t) for t in range(PACK)]
+        ups = [sbuf([P, S], F32, "up%d" % t) for t in range(PACK)]
+        results = [sbuf([P, S], F32, "result%d" % t) for t in range(PACK)]
 
-        pieces = {0: halves, 1: (whole,), 2: (whole,), 3: halves}
-        pending = None
-        for t in range(PACK):
-            if t + 1 < PACK:
-                fetch(t + 1)
-            down = sb([P, S], F32, "down%d" % t)
-            up = sb([P, S], F32, "up%d" % t)
-            hinge = sb([P, S], F32, "hinge%d" % t)
-            result = sb([P, S], F32, "result%d" % t)
-            for part in pieces[t]:
+        def gather_less_h(t, name, values, parts):
+            for part in parts:
                 nc.vector.tensor_tensor(
-                    down[:, part], windows[t][:].indirect(entries(lists["n3"], part)), plains[t][:, part], ALU.subtract
+                    values[:, part], windows[t][:].indirect(entries(lists[name], part)), plains[t][:, part], ALU.subtract
                 )
-            nc.scalar.activation(hinge[:], down[:], ACT.Relu, scale=-2.0)
 
-            rise = sb([P, S], F32, "rise%d" % t)
+        def turned_relu(values, scale, number, name):
+            turned = bank(number, S, name + "_turned")
+            for block in BLOCKS:
+                nc.tensor.transpose(turned[:, block], values[:, block], identity[:])
+            hinge = sbuf([P, S], F32, name)
+            nc.scalar.activation(hinge[:], turned[:], ACT.Relu, scale=scale)
+            return hinge
 
-            def finish(part, t=t, up=up, hinge=hinge, result=result, rise=rise):
-                if t + 1 < PACK:
-                    nc.vector.tensor_tensor(result[:, part], rise[:, part], hinge[:, part], ALU.add)
-                else:
-                    nc.vector.scalar_tensor_tensor(result[:, part], up[:, part], 0.0, hinge[:, part], ALU.max, ALU.add)
-                nc.sync.dma_start(out_rows[t][:, part], result[:, part])
+        def turned_sum(fall, rise, number, name):
+            total = bank(number, S, name)
+            for block in BLOCKS:
+                nc.tensor.matmul(total[:, block], fall[:, block], identity[:], start=True, stop=False, is_transpose=True)
+                nc.tensor.matmul(total[:, block], rise[:, block], identity[:], start=False, stop=True, is_transpose=True)
+            return total
 
-            if pending is not None:
-                pending(whole)
-            if t + 1 < PACK:
-                for part in pieces[t]:
-                    nc.vector.tensor_tensor(
-                        up[:, part], windows[t][:].indirect(entries(lists["n4"], part)), plains[t][:, part], ALU.subtract
-                    )
-                nc.scalar.activation(rise[:], up[:], ACT.Relu)
-                pending = finish
-            else:
-                tail = (halves[0], third, last)
-                for i, part in enumerate(tail):
-                    nc.vector.tensor_tensor(
-                        up[:, part], windows[t][:].indirect(entries(lists["n4"], part)), plains[t][:, part], ALU.subtract
-                    )
-                    if i > 0:
-                        finish(tail[i - 1])
-                finish(last)
+        def store_bank(t, total):
+            nc.scalar.activation(results[t][:], total[:], ACT.Copy)
+            nc.sync.dma_start(out_rows[t], results[t][:])
+
+        def plain_relu(values, scale, name):
+            hinge = sbuf([P, S], F32, name)
+            nc.scalar.activation(hinge[:], values[:], ACT.Relu, scale=scale)
+            return hinge
+
+        gather_less_h(0, "n3", downs[0], HALVES)
+        gather_less_h(0, "n4", ups[0], HALVES)
+        fall0 = turned_relu(downs[0], -2.0, 6, "fall0")
+        rise0 = turned_relu(ups[0], 1.0, 7, "rise0")
+        gather_less_h(1, "n3", downs[1], (WHOLE,))
+        gather_less_h(1, "n4", ups[1], (WHOLE,))
+        fall1 = turned_relu(downs[1], -2.0, 0, "fall1")
+        total0 = turned_sum(fall0, rise0, 1, "total0")
+        rise1 = turned_relu(ups[1], 1.0, 2, "rise1")
+        gather_less_h(2, "n3", downs[2], (WHOLE,))
+        gather_less_h(2, "n4", ups[2], (WHOLE,))
+        fall2 = plain_relu(downs[2], -2.0, "fall2")
+        store_bank(0, total0)
+        total1 = turned_sum(fall1, rise1, 6, "total1")
+        rise2 = plain_relu(ups[2], 1.0, "rise2")
+        store_bank(1, total1)
+
+        gather_less_h(3, "n3", downs[3], HALVES)
+        fall3 = plain_relu(downs[3], -2.0, "fall3")
+        nc.vector.tensor_tensor(results[2][:], rise2[:], fall2[:], ALU.add)
+        nc.sync.dma_start(out_rows[2], results[2][:])
+
+        def finish_last_tile(part):
+            nc.vector.scalar_tensor_tensor(results[3][:, part], ups[3][:, part], 0.0, fall3[:, part], ALU.max, ALU.add)
+            nc.sync.dma_start(out_rows[3][:, part], results[3][:, part])
+
+        for i, part in enumerate(TAPER):
+            gather_less_h(3, "n4", ups[3], (part,))
+            if i > 0:
+                finish_last_tile(TAPER[i - 1])
+        finish_last_tile(LAST_QUARTER)

from contextlib import ExitStack

import concourse.mybir as mybir
from concourse.masks import make_identity

K, T, S, H, J, G = 512, 2048, 512, 512, 512, 2048
FLOPS = 2 * K * H * S + 2 * H * H * S

F32 = mybir.dt.float32
BF16 = mybir.dt.bfloat16
I32 = mybir.dt.int32
U32 = mybir.dt.uint32
U16 = mybir.dt.uint16
U8 = mybir.dt.uint8
FP8X4 = mybir.dt.float8_e4m3fn_x4
ALU = mybir.AluOpType
ACT = mybir.ActivationFunctionType

P = 128
PACK = 4
GROUP = 16
LINE = 4

WHOLE = slice(0, S)
FIRST_HALF = slice(0, S // 2)
SECOND_HALF = slice(S // 2, S)
THIRD_QUARTER = slice(S // 2, 3 * S // 4)
LAST_QUARTER = slice(3 * S // 4, S)
HALVES = (FIRST_HALF, SECOND_HALF)
TAPER = (FIRST_HALF, THIRD_QUARTER, LAST_QUARTER)
BLOCKS = tuple(slice(c * P, (c + 1) * P) for c in range(S // P))

HALF_H_SCALE = 0.0625 * 0.5


def width(part):
    return part.stop - part.start


def entries(offsets, part):
    return offsets[:, part.start // GROUP : part.stop // GROUP]


def tile_picked_densekinddhinge_none_p_kernel(
    tc, x_words, x_scales, w1, tab, gs, d_words, d_scales, offs, n1, n2, k1, n3, n4, out
):
    nc = tc.nc
    with ExitStack() as ctx:
        keep = ctx.enter_context(tc.tile_pool(name="keep", bufs=1))
        psum = ctx.enter_context(tc.psum_pool(name="psum", bufs=1))

        def sbuf(shape, dtype, name, slot=None):
            return keep.tile(shape, dtype, name=name, tag=slot or name, align_bytes=64)

        def bank(number, columns, name):
            return psum.tile([P, columns], F32, name=name, tag="bank%d" % number)

        def product(acc, stationary, stationary_plane, moving, moving_plane):
            nc.tensor.matmul_mx(
                out=acc,
                lhsT=stationary.bitcast(FP8X4),
                lhsT_scale=stationary_plane,
                rhs=moving.bitcast(FP8X4),
                rhs_scale=moving_plane,
                start=True,
                stop=True,
            )

        lists = {}

        def load_list(name, dram):
            lists[name] = sbuf([P, S // GROUP], U16, name + "_list")
            nc.sync.dma_start(lists[name][:], dram)

        x_bytes = sbuf([P, T], U8, "x_bytes")
        d_bytes = sbuf([P, G], U8, "d_bytes")
        d_plane = sbuf([P, H], U8, "d_plane")
        for table_bytes in (x_bytes, d_bytes):
            nc.gpsimd.memset(table_bytes[:, : T // 2].bitcast(I32), 0)
            nc.vector.memset(table_bytes[:, T // 2 :].bitcast(I32), 0)
        nc.gpsimd.memset(d_plane[:].bitcast(I32), 0)
        identity = sbuf([P, P], F32, "identity")
        make_identity(nc, identity[:])

        w_raw = sbuf([P, PACK, H], F32, "w_raw")
        x_table = sbuf([P, T], U32, "x_table")
        d_table = sbuf([P, G], U32, "d_table")
        gain = sbuf([P, PACK], F32, "gain")
        tabs = [sbuf([P, J], F32, "tab%d" % t) for t in range(PACK)]

        load_list("offs", offs)
        load_list("k1", k1)
        x_rows = x_scales[0].rearrange("(q a) c -> a q c", a=4)
        for a in range(4):
            nc.sync.dma_start(x_bytes[a:P:32, :].bitcast(I32), x_rows[a].bitcast(I32))
        nc.sync.dma_start(d_bytes[0:P:8, :].bitcast(I32), d_scales[0].bitcast(I32))
        nc.sync.dma_start(w_raw[:], w1.rearrange("(p j) c -> p j c", j=PACK))
        nc.sync.dma_start(x_table[:].bitcast(I32), x_words[0].rearrange("p n t -> p (n t)").bitcast(I32))
        load_list("n1", n1)
        load_list("n2", n2)
        tab_rows = tab.rearrange("(p t) c -> t p c", t=PACK)
        for t in range(PACK):
            nc.sync.dma_start(tabs[t][:], tab_rows[t])
        nc.sync.dma_start(gain[:], gs.rearrange("(p t) o -> p (t o)", t=PACK))
        nc.sync.dma_start(d_table[:].bitcast(I32), d_words[0].rearrange("p n t -> p (n t)").bitcast(I32))
        load_list("n3", n3)
        load_list("n4", n4)

        x_plane = sbuf([P, S], U8, "x_plane")
        nc.vector.tensor_copy(x_plane[:], x_bytes[:].indirect(lists["offs"][:]))

        d_picked_bytes = sbuf([P, H], U8, "d_picked_bytes", "before_w_cast")
        nc.vector.tensor_copy(d_picked_bytes[:], d_bytes[:].indirect(lists["k1"][:]))
        d_dealt_bytes = sbuf([P, H], U8, "d_dealt_bytes")
        nc.vector.tensor_copy(
            d_dealt_bytes[:].rearrange("p (t m) -> p t m", t=PACK),
            d_picked_bytes[:].rearrange("p (m t) -> p t m", t=PACK),
        )

        w_src = w_raw[:].rearrange("p j (m t) -> p m t j", t=PACK)
        w_bfs = [sbuf([P, 2 * H], BF16, "w_bf0", "before_w_cast"), sbuf([P, 2 * H], BF16, "w_bf1")]
        w_dsts = [w_bf[:].rearrange("p (t m j) -> p m t j", t=2, j=PACK) for w_bf in w_bfs]
        nc.vector.tensor_copy(w_dsts[0], w_src[:, :, 0:2, :])
        nc.scalar.activation(w_dsts[1], w_src[:, :, 2:4, :], ACT.Copy)

        w_codes = sbuf([P, H], U32, "w_codes")
        w_plane = sbuf([P, H], U8, "w_plane")
        x_codes = sbuf([P, S], U32, "x_codes")
        nc.vector.quantize_mx(out=w_codes[:, FIRST_HALF].bitcast(FP8X4), scales=w_plane[:, FIRST_HALF], in_=w_bfs[0][:])
        for part in HALVES:
            nc.vector.tensor_copy(x_codes[:, part], x_table[:].indirect(entries(lists["offs"], part)))
        nc.vector.quantize_mx(out=w_codes[:, SECOND_HALF].bitcast(FP8X4), scales=w_plane[:, SECOND_HALF], in_=w_bfs[1][:])

        for a in range(4):
            nc.sync.dma_start(d_plane[a:P:32, :].bitcast(I32), d_dealt_bytes[8 * a : P : 32, :].bitcast(I32))

        ys = [sbuf([P, S], F32, "y%d" % t) for t in range(PACK)]
        for pair in range(2):
            for c, part in enumerate(HALVES):
                for t in (2 * pair, 2 * pair + 1):
                    acc = bank(2 * t + c, width(part), "y_acc%d_%d" % (t, c))
                    product(acc[:], w_codes[:, BLOCKS[t]], w_plane[:, BLOCKS[t]], x_codes[:, part], x_plane[:, part])
                    nc.scalar.activation(ys[t][:, part], acc[:], ACT.Copy)

        z_codes = sbuf([P, S], U32, "z_codes")
        z_plane = sbuf([P, S], U8, "z_plane")
        z = sbuf([P, PACK, S], F32, "z")
        z_bf = sbuf([P, PACK * S], BF16, "z_bf")

        def make_z(pair, part, slot=None):
            name = "_%d_%d" % (pair, part.start)
            less_y = sbuf([P, 2, width(part)], F32, "less_y" + name, slot)
            diff = sbuf([P, 2, width(part)], F32, "diff" + name)
            size = sbuf([P, 2, width(part)], F32, "size" + name)
            for u in range(2):
                t = 2 * pair + u
                nc.vector.tensor_tensor(
                    less_y[:, u, :], tabs[t][:].indirect(entries(lists["n1"], part)), ys[t][:, part], ALU.subtract
                )
            for u in range(2):
                t = 2 * pair + u
                nc.vector.tensor_tensor(
                    diff[:, u, :], ys[t][:].indirect(entries(lists["n2"], part)), less_y[:, u, :], ALU.add
                )
            nc.scalar.activation(size[:], diff[:], ACT.Abs)
            for u in range(2):
                t = 2 * pair + u
                nc.scalar.activation(z[:, t, part], size[:, u, :], ACT.Copy, scale=gain[:, t : t + 1])

        def round_z(part):
            nc.scalar.copy(
                z_bf[:, PACK * part.start : PACK * part.stop].rearrange("p (c i t) -> p c t i", i=LINE, t=PACK),
                z[:, :, part].rearrange("p t (c i) -> p c t i", i=LINE),
            )

        def quantise_z(part):
            nc.vector.quantize_mx(
                out=z_codes[:, part].bitcast(FP8X4),
                scales=z_plane[:, part],
                in_=z_bf[:, PACK * part.start : PACK * part.stop],
            )

        make_z(0, FIRST_HALF)
        make_z(1, FIRST_HALF)
        round_z(FIRST_HALF)
        make_z(0, SECOND_HALF)
        make_z(1, THIRD_QUARTER, "before_d_words")
        round_z(THIRD_QUARTER)
        make_z(1, LAST_QUARTER)
        round_z(LAST_QUARTER)

        d_picked_words = sbuf([P, H], U32, "d_picked_words", "before_d_words")
        nc.vector.tensor_copy(d_picked_words[:], d_table[:].indirect(lists["k1"][:]))
        quantise_z(FIRST_HALF)
        d_codes = sbuf([P, H], U32, "d_codes")
        deal_dst = d_codes[:].bitcast(I32).rearrange("p (t c i) -> p c t i", t=PACK, i=LINE)
        deal_src = d_picked_words[:].bitcast(I32).rearrange("p (c i t) -> p c t i", t=PACK, i=LINE)
        nc.vector.tensor_copy(deal_dst[:, :, 0:1, :], deal_src[:, :, 0:1, :])
        quantise_z(THIRD_QUARTER)
        quantise_z(LAST_QUARTER)
        nc.vector.tensor_copy(deal_dst[:, :, 1:PACK, :], deal_src[:, :, 1:PACK, :])

        out_rows = out.rearrange("(p t) c -> t p c", t=PACK)
        wide = {t: sbuf([P, 2 * S], F32, "h_wide%d" % t) for t in (1, 2)}
        windows = [sbuf([P, S], F32, "h_window0"), wide[1], wide[2], sbuf([P, S], F32, "h_window3")]
        plain2 = sbuf([P, S], F32, "h_plain2")
        plain3 = sbuf([P, S], F32, "h_plain3")
        plains = [wide[1][:, S:], wide[2][:, S:], plain2[:], plain3[:]]

        def second_product(t, part, number):
            acc = bank(number, width(part), "h_acc%d_%d" % (t, part.start))
            product(acc[:], d_codes[:, BLOCKS[t]], d_plane[:, BLOCKS[t]], z_codes[:, part], z_plane[:, part])
            return acc

        first_accs = [second_product(0, part, number) for number, part in enumerate(TAPER)]
        for part, acc in zip(TAPER[:2], first_accs):
            nc.scalar.activation(windows[0][:, part], acc[:], ACT.Copy, scale=HALF_H_SCALE)
        nc.vector.tensor_scalar(windows[0][:, LAST_QUARTER], first_accs[2][:], HALF_H_SCALE, None, ALU.mult)
        for part, acc in zip(TAPER, first_accs):
            nc.scalar.activation(plains[0][:, part], acc[:], ACT.Copy, scale=HALF_H_SCALE)
        for t in range(1, PACK):
            acc = second_product(t, WHOLE, 2 + t)
            nc.scalar.activation(windows[t][:, WHOLE], acc[:], ACT.Copy, scale=HALF_H_SCALE)
            nc.scalar.activation(plains[t], acc[:], ACT.Copy, scale=HALF_H_SCALE)

        downs = [sbuf([P, S], F32, "down%d" % t) for t in range(PACK)]
        ups = [sbuf([P, S], F32, "up%d" % t) for t in range(PACK)]
        results = [sbuf([P, S], F32, "result%d" % t) for t in range(PACK)]

        def gather_less_h(t, name, values, parts):
            for part in parts:
                nc.vector.tensor_tensor(
                    values[:, part], windows[t][:].indirect(entries(lists[name], part)), plains[t][:, part], ALU.subtract
                )

        def turned_relu(values, scale, number, name):
            turned = bank(number, S, name + "_turned")
            for block in BLOCKS:
                nc.tensor.transpose(turned[:, block], values[:, block], identity[:])
            hinge = sbuf([P, S], F32, name)
            nc.scalar.activation(hinge[:], turned[:], ACT.Relu, scale=scale)
            return hinge

        def turned_sum(fall, rise, number, name):
            total = bank(number, S, name)
            for block in BLOCKS:
                nc.tensor.matmul(total[:, block], fall[:, block], identity[:], start=True, stop=False, is_transpose=True)
                nc.tensor.matmul(total[:, block], rise[:, block], identity[:], start=False, stop=True, is_transpose=True)
            return total

        def store_bank(t, total):
            nc.scalar.activation(results[t][:], total[:], ACT.Copy)
            nc.sync.dma_start(out_rows[t], results[t][:])

        def plain_relu(values, scale, name):
            hinge = sbuf([P, S], F32, name)
            nc.scalar.activation(hinge[:], values[:], ACT.Relu, scale=scale)
            return hinge

        gather_less_h(0, "n3", downs[0], HALVES)
        gather_less_h(0, "n4", ups[0], HALVES)
        fall0 = turned_relu(downs[0], -2.0, 6, "fall0")
        rise0 = turned_relu(ups[0], 1.0, 7, "rise0")
        gather_less_h(1, "n3", downs[1], (WHOLE,))
        gather_less_h(1, "n4", ups[1], (WHOLE,))
        fall1 = turned_relu(downs[1], -2.0, 0, "fall1")
        total0 = turned_sum(fall0, rise0, 1, "total0")
        rise1 = turned_relu(ups[1], 1.0, 2, "rise1")
        gather_less_h(2, "n3", downs[2], (WHOLE,))
        gather_less_h(2, "n4", ups[2], (WHOLE,))
        fall2 = plain_relu(downs[2], -2.0, "fall2")
        store_bank(0, total0)
        total1 = turned_sum(fall1, rise1, 6, "total1")
        rise2 = plain_relu(ups[2], 1.0, "rise2")
        store_bank(1, total1)

        gather_less_h(3, "n3", downs[3], HALVES)
        fall3 = plain_relu(downs[3], -2.0, "fall3")
        nc.vector.tensor_tensor(results[2][:], rise2[:], fall2[:], ALU.add)
        nc.sync.dma_start(out_rows[2], results[2][:])

        def finish_last_tile(part):
            nc.vector.scalar_tensor_tensor(results[3][:, part], ups[3][:, part], 0.0, fall3[:, part], ALU.max, ALU.add)
            nc.sync.dma_start(out_rows[3][:, part], results[3][:, part])

        for i, part in enumerate(TAPER):
            gather_less_h(3, "n4", ups[3], (part,))
            if i > 0:
                finish_last_tile(TAPER[i - 1])
        finish_last_tile(LAST_QUARTER)
